import numpy as np, ml_dtypes
CORES = [72,73,74,75,204,205,206,207]
N = 8
def setup_inputs(rng):
    return {"x": rng.standard_normal((N, 128, 2048), dtype=np.float32).astype(ml_dtypes.bfloat16)}
def reference(x):
    s = x.max(axis=0)
    b = 2048 // N
    return {"y": np.stack([s[:, r * b:(r + 1) * b] for r in range(N)])}

@@ -1,0 +1,77 @@
+from concourse.bass import DstId, RemoteDMATransfer
+
+NB = 8
+W = 256
+MAX = 2
+
+SCRATCH = {
+    "xs":   ("sbuf", [128, NB * W], "bfloat16"),
+    "land": ("sbuf", [128, 4 * W], "bfloat16"),
+    "part": ("sbuf", [128, W], "bfloat16"),
+    "res":  ("sbuf", [128, W], "bfloat16"),
+}
+SEMAPHORES = ["ldf", "ldn", "arr", "done", "sent", "st"]
+
+
+def plan(T):
+    chips = []
+    for k in (0, 1):
+        ranks = list(T.cores[4 * k:4 * k + 4])
+        base = ranks[0] - ranks[0] % 8
+        helpers = [c for c in range(base, base + 8) if c not in ranks]
+        own = list(range(4 * k, 4 * k + 4))
+        far = list(range(4 * (1 - k), 4 * (1 - k) + 4))
+        folder = {far[2]: ranks[0], far[3]: ranks[1], own[0]: ranks[2], own[1]: ranks[3],
+                  own[2]: helpers[0], own[3]: helpers[1], far[0]: helpers[2], far[1]: helpers[3]}
+        chips.append({"ranks": ranks, "helpers": helpers, "own": own, "far": far, "folder": folder})
+    return chips
+
+
+def rank_program(g, core, T, topo):
+    chips = plan(T)
+    mine = [k for k in (0, 1) if core in chips[k]["ranks"] or core in chips[k]["helpers"]]
+    if not mine:
+        return
+    me, other = chips[mine[0]], chips[1 - mine[0]]
+    rank = T.rank_of(core)
+    block = [j for j in range(NB) if me["folder"][j] == core][0]
+    sent = 0
+
+    def dst_id(d):
+        rid, pid = topo.addr(d, core)
+        return DstId(rid=rid, pnc=pid)
+
+    def col(t, i):
+        return t[:, i * W:(i + 1) * W]
+
+    if rank is not None:
+        slot = me["ranks"].index(core)
+        f0, n0 = me["far"][0] * W, me["own"][0] * W
+        g.sync.dma_start(T.xs[:, f0:f0 + 4 * W], T.x[:, f0:f0 + 4 * W]).then_inc(T.sem.ldf, 16)
+        g.scalar.dma_start(T.xs[:, n0:n0 + 4 * W], T.x[:, n0:n0 + 4 * W]).then_inc(T.sem.ldn, 16)
+        for sem, blocks in ((T.sem.ldf, me["far"]), (T.sem.ldn, me["own"])):
+            g.wait_ge(sem, 16)
+            trs = [RemoteDMATransfer(dst_ids=[dst_id(me["folder"][j])], dma_engine_mask=0xF << (4 * i),
+                                     remote_sem=T.sem.arr, src=col(T.xs, j), dst=col(T.land, slot))
+                   for i, j in enumerate(blocks) if me["folder"][j] != core]
+            g.remote_dma_fused(trs, local_sem=T.sem.sent)
+            sent += 4 * len(trs)
+
+    srcs = [col(T.xs, block) if c == core else col(T.land, i) for i, c in enumerate(me["ranks"])]
+    expect = 4 * sum(1 for c in me["ranks"] if c != core)
+    if block in me["far"]:
+        target, where, sem, mask, n = other["folder"][block], T.part, T.sem.arr, 0x00FF, 8
+    else:
+        srcs.append(T.part[:, :])
+        expect += 8
+        target, where, sem, mask, n = T.cores[block], T.res, T.sem.done, 0xFFFF, 16
+    g.wait_ge(T.sem.arr, expect)
+    g.remote_dma_fused([RemoteDMATransfer(dst_ids=[dst_id(target)], dma_engine_mask=mask, remote_sem=sem,
+                                          srcs=srcs, dsts=[where[:, :]], alu_op=MAX)], local_sem=T.sem.sent)
+    sent += n
+
+    if rank is not None:
+        g.sync.wait_ge(T.sem.done, 16)
+        g.sync.dma_start(T.y[:, :], T.res[:, :]).then_inc(T.sem.st, 16)
+        g.wait_ge(T.sem.st, 16)
+    g.wait_ge(T.sem.sent, sent)

@@ -5,10 +5,10 @@ W = 256
 MAX = 2
 
 SCRATCH = {
-    "xs":   ("sbuf", [128, NB * W], "bfloat16"),
-    "land": ("sbuf", [128, 4 * W], "bfloat16"),
-    "part": ("sbuf", [128, W], "bfloat16"),
-    "res":  ("sbuf", [128, W], "bfloat16"),
+    "xs":   ("dram", [NB, 128, W], "bfloat16"),
+    "land": ("dram", [4, 128, W], "bfloat16"),
+    "part": ("dram", [128, W], "bfloat16"),
+    "res":  ("dram", [128, W], "bfloat16"),
 }
 SEMAPHORES = ["ldf", "ldn", "arr", "done", "sent", "st"]
 
@@ -41,23 +41,22 @@ def rank_program(g, core, T, topo):
         rid, pid = topo.addr(d, core)
         return DstId(rid=rid, pnc=pid)
 
-    def col(t, i):
-        return t[:, i * W:(i + 1) * W]
-
     if rank is not None:
         slot = me["ranks"].index(core)
-        f0, n0 = me["far"][0] * W, me["own"][0] * W
-        g.sync.dma_start(T.xs[:, f0:f0 + 4 * W], T.x[:, f0:f0 + 4 * W]).then_inc(T.sem.ldf, 16)
-        g.scalar.dma_start(T.xs[:, n0:n0 + 4 * W], T.x[:, n0:n0 + 4 * W]).then_inc(T.sem.ldn, 16)
-        for sem, blocks in ((T.sem.ldf, me["far"]), (T.sem.ldn, me["own"])):
-            g.wait_ge(sem, 16)
+        halves = ((T.sem.ldf, me["far"]), (T.sem.ldn, me["own"]))
+        for sem, blocks in halves:
+            for i, j in enumerate(blocks):
+                q = g.sync if i % 2 == 0 else g.scalar
+                q.dma_start(T.xs[j], T.x[:, j * W:(j + 1) * W]).then_inc(sem, 16)
+        for sem, blocks in halves:
+            g.wait_ge(sem, 16 * len(blocks))
             trs = [RemoteDMATransfer(dst_ids=[dst_id(me["folder"][j])], dma_engine_mask=0xF << (4 * i),
-                                     remote_sem=T.sem.arr, src=col(T.xs, j), dst=col(T.land, slot))
+                                     remote_sem=T.sem.arr, src=T.xs[j], dst=T.land[slot])
                    for i, j in enumerate(blocks) if me["folder"][j] != core]
             g.remote_dma_fused(trs, local_sem=T.sem.sent)
             sent += 4 * len(trs)
 
-    srcs = [col(T.xs, block) if c == core else col(T.land, i) for i, c in enumerate(me["ranks"])]
+    srcs = [T.xs[block] if c == core else T.land[i] for i, c in enumerate(me["ranks"])]
     expect = 4 * sum(1 for c in me["ranks"] if c != core)
     if block in me["far"]:
         target, where, sem, mask, n = other["folder"][block], T.part, T.sem.arr, 0x00FF, 8

from concourse.bass import DstId, RemoteDMATransfer

NB = 8
W = 256
MAX = 2

SCRATCH = {
    "xs":   ("dram", [NB, 128, W], "bfloat16"),
    "land": ("dram", [4, 128, W], "bfloat16"),
    "part": ("dram", [128, W], "bfloat16"),
    "res":  ("dram", [128, W], "bfloat16"),
}
SEMAPHORES = ["ldf", "ldn", "arr", "done", "sent", "st"]


def plan(T):
    chips = []
    for k in (0, 1):
        ranks = list(T.cores[4 * k:4 * k + 4])
        base = ranks[0] - ranks[0] % 8
        helpers = [c for c in range(base, base + 8) if c not in ranks]
        own = list(range(4 * k, 4 * k + 4))
        far = list(range(4 * (1 - k), 4 * (1 - k) + 4))
        folder = {far[2]: ranks[0], far[3]: ranks[1], own[0]: ranks[2], own[1]: ranks[3],
                  own[2]: helpers[0], own[3]: helpers[1], far[0]: helpers[2], far[1]: helpers[3]}
        chips.append({"ranks": ranks, "helpers": helpers, "own": own, "far": far, "folder": folder})
    return chips


def rank_program(g, core, T, topo):
    chips = plan(T)
    mine = [k for k in (0, 1) if core in chips[k]["ranks"] or core in chips[k]["helpers"]]
    if not mine:
        return
    me, other = chips[mine[0]], chips[1 - mine[0]]
    rank = T.rank_of(core)
    block = [j for j in range(NB) if me["folder"][j] == core][0]
    sent = 0

    def dst_id(d):
        rid, pid = topo.addr(d, core)
        return DstId(rid=rid, pnc=pid)

    if rank is not None:
        slot = me["ranks"].index(core)
        halves = ((T.sem.ldf, me["far"]), (T.sem.ldn, me["own"]))
        for sem, blocks in halves:
            for i, j in enumerate(blocks):
                q = g.sync if i % 2 == 0 else g.scalar
                q.dma_start(T.xs[j], T.x[:, j * W:(j + 1) * W]).then_inc(sem, 16)
        for sem, blocks in halves:
            g.wait_ge(sem, 16 * len(blocks))
            trs = [RemoteDMATransfer(dst_ids=[dst_id(me["folder"][j])], dma_engine_mask=0xF << (4 * i),
                                     remote_sem=T.sem.arr, src=T.xs[j], dst=T.land[slot])
                   for i, j in enumerate(blocks) if me["folder"][j] != core]
            g.remote_dma_fused(trs, local_sem=T.sem.sent)
            sent += 4 * len(trs)

    srcs = [T.xs[block] if c == core else T.land[i] for i, c in enumerate(me["ranks"])]
    expect = 4 * sum(1 for c in me["ranks"] if c != core)
    if block in me["far"]:
        target, where, sem, mask, n = other["folder"][block], T.part, T.sem.arr, 0x00FF, 8
    else:
        srcs.append(T.part[:, :])
        expect += 8
        target, where, sem, mask, n = T.cores[block], T.res, T.sem.done, 0xFFFF, 16
    g.wait_ge(T.sem.arr, expect)
    g.remote_dma_fused([RemoteDMATransfer(dst_ids=[dst_id(target)], dma_engine_mask=mask, remote_sem=sem,
                                          srcs=srcs, dsts=[where[:, :]], alu_op=MAX)], local_sem=T.sem.sent)
    sent += n

    if rank is not None:
        g.sync.wait_ge(T.sem.done, 16)
        g.sync.dma_start(T.y[:, :], T.res[:, :]).then_inc(T.sem.st, 16)
        g.wait_ge(T.sem.st, 16)
    g.wait_ge(T.sem.sent, sent)
